import numpy as np
CORES = [32,33,34,35,36,37,38,39,40,41,42,43,44,45,46,47,48,49,50,51,52,53,54,55,56,57,58,59,60,61,62,63]
N = 32
PERM = [[0,25],[1,28],[2,20],[3,19],[4,5],[5,3],[6,7],[7,22],[8,1],[9,12],[10,26],[11,0],[12,6],[13,8],[14,14],[15,21],[16,4],[17,11],[18,30],[19,17],[20,9],[21,29],[22,10],[23,2],[24,23],[25,24],[26,15],[27,18],[28,31],[29,13],[30,27],[31,16]]
def setup_inputs(rng):
    return {"x": rng.standard_normal((N, 128, 1024), dtype=np.float32)}
def reference(x):
    y = np.empty_like(x)
    for s, d in PERM:
        y[d] = x[s]
    return {"y": y}

@@ -1,0 +1,157 @@
+import comms_topo
+
+UNITS = 8
+UROWS = 128 // UNITS
+UCOLS = 1024 // UNITS
+BASE = 32
+DEST = [25, 28, 20, 19, 5, 3, 7, 22, 1, 12, 26, 0, 6, 8, 14, 21, 4, 11, 30, 17, 9, 29, 10, 2, 23, 24, 15, 18, 31, 13,
+        27, 16]
+
+
+def C(chip, k):
+    return chip * 8 + k
+
+
+Q = 2
+D = (Q, ())
+H = (2 * Q, ())
+
+
+def V(chip, k):
+    return (Q, (C(chip, k),))
+
+
+ROUTES = {
+    0: [V(4, 6), V(4, 2), V(4, 6), V(4, 7)],
+    1: [V(4, 3), V(4, 6), V(4, 3), V(4, 6)],
+    2: [D, D, D, D],
+    3: [V(4, 4), D, D, D],
+    4: [H, H],
+    5: [H, H],
+    6: [H, H],
+    7: [D, D, D, D],
+    8: [V(5, 2), V(5, 3), V(5, 7), V(5, 2)],
+    9: [H, H],
+    10: [D, D, D, D],
+    11: [D, D, D, D],
+    12: [V(5, 6), V(5, 6), V(5, 6), V(5, 6)],
+    13: [H, H],
+    15: [V(7, 2), D, V(7, 2), D],
+    16: [D, D, D, D],
+    17: [V(4, 2), V(6, 3), V(4, 3), V(4, 2)],
+    18: [D, D, D, D],
+    19: [H, H],
+    20: [V(4, 3), V(6, 3), V(4, 6), V(6, 3)],
+    21: [V(6, 6), V(6, 7), V(6, 6), V(6, 7)],
+    22: [V(4, 7), D, D, D],
+    23: [D, D, D, D],
+    24: [V(7, 6), V(7, 3), V(7, 6), V(7, 6)],
+    25: [H, H],
+    26: [D, D, D, D],
+    27: [D, D, D, D],
+    28: [H, H],
+    29: [D, D, D, D],
+    30: [H, H],
+    31: [D, D, D, D],
+}
+
+T_LOAD = 0.5
+T_CHIP = (1.0, 0.25)
+T_LINK = (1.5, 0.75)
+
+
+def engines(src, dst):
+    return comms_topo.mask(src, dst)
+
+
+def popcount(m):
+    return bin(m).count("1")
+
+
+def build():
+    nbuf = {}
+    nsem = {}
+    loads, sends, stores = {}, {}, {}
+    widths = {}
+
+    def buf(core, n):
+        i = nbuf.get((core, n), 0)
+        nbuf[(core, n)] = i + 1
+        widths[n] = max(widths.get(n, 0), i + 1)
+        return "b%d_%d" % (n, i)
+
+    def sem(core):
+        i = nsem.get(core, 0)
+        nsem[core] = i + 1
+        return "s%d" % i
+
+    order = 0
+    for s in range(len(DEST)):
+        src, dst = BASE + s, BASE + DEST[s]
+        if src == dst:
+            continue
+        off = 0
+        for n, relays in ROUTES[s]:
+            path = [src] + list(relays) + [dst]
+            p = {"off": off, "n": n, "path": path,
+                 "buf": [buf(c, n) for c in path], "sem": [sem(c) for c in path], "cnt": [16], "t": []}
+            off += n
+            t = T_LOAD * off
+            p["t"].append(t)
+            for h in range(len(path) - 1):
+                a, b = path[h], path[h + 1]
+                p["cnt"].append(popcount(engines(a, b)))
+                fix, per = T_CHIP if comms_topo.chip(a) == comms_topo.chip(b) else T_LINK
+                sends.setdefault(a, []).append((t, order, p, h))
+                t += fix + per * n
+                p["t"].append(t)
+            loads.setdefault(src, []).append(p)
+            stores.setdefault(dst, []).append((t, order, p))
+            order += 1
+        if off != UNITS:
+            raise ValueError("rank %d: pieces do not add up to a message" % s)
+    for table in (sends, stores):
+        for c in table:
+            table[c].sort(key=lambda e: (e[0], e[1]))
+    scratch = {}
+    for n in widths:
+        for i in range(widths[n]):
+            scratch["b%d_%d" % (n, i)] = ("dram", [128, n * UCOLS], "float32")
+    sems = ["s%d" % i for i in range(max(nsem.values()))] + ["sent", "stored"]
+    return loads, sends, stores, scratch, sems
+
+
+LOADS, SENDS, STORES, SCRATCH, SEMAPHORES = build()
+
+
+def rank_program(g, core, T, topo):
+    rank = T.rank_of(core)
+    if rank is None:
+        return
+    for s, d in T.tables["PERM"]:
+        if DEST[s] != d:
+            raise ValueError("ROUTES were laid out for another permutation")
+    queues = (g.sync, g.scalar)
+    stored = 0
+    if DEST[rank] == rank:
+        g.sync.dma_start(T.y[:], T.x[:]).then_inc(T.sem.stored, 16)
+        stored += 16
+    for i, p in enumerate(LOADS.get(core, [])):
+        r0 = p["off"] * UROWS
+        queues[i % 2].dma_start(T[p["buf"][0]][:], T.x[r0:r0 + p["n"] * UROWS, :]).then_inc(T.sem[p["sem"][0]], 16)
+    sent = 0
+    for t, o, p, h in SENDS.get(core, []):
+        nxt = p["path"][h + 1]
+        rid, pid, se = topo.addr(nxt)
+        m = engines(core, nxt)
+        g.wait_ge(T.sem[p["sem"][h]], p["cnt"][h])
+        g.remote_dma(T[p["buf"][h + 1]][:], T[p["buf"][h]][:], T.sem[p["sem"][h + 1]], T.sem.sent, pid, rid, m)
+        sent += popcount(m)
+    for i, (t, o, p) in enumerate(STORES.get(core, [])):
+        r0 = p["off"] * UROWS
+        q = queues[i % 2]
+        q.wait_ge(T.sem[p["sem"][-1]], p["cnt"][-1])
+        q.dma_start(T.y[r0:r0 + p["n"] * UROWS, :], T[p["buf"][-1]][:]).then_inc(T.sem.stored, 16)
+        stored += 16
+    g.wait_ge(T.sem.sent, sent)
+    g.wait_ge(T.sem.stored, stored)

@@ -6,54 +6,21 @@ UCOLS = 1024 // UNITS
 BASE = 32
 DEST = [25, 28, 20, 19, 5, 3, 7, 22, 1, 12, 26, 0, 6, 8, 14, 21, 4, 11, 30, 17, 9, 29, 10, 2, 23, 24, 15, 18, 31, 13,
         27, 16]
-
-
-def C(chip, k):
-    return chip * 8 + k
-
-
-Q = 2
-D = (Q, ())
-H = (2 * Q, ())
-
-
-def V(chip, k):
-    return (Q, (C(chip, k),))
-
-
 ROUTES = {
-    0: [V(4, 6), V(4, 2), V(4, 6), V(4, 7)],
-    1: [V(4, 3), V(4, 6), V(4, 3), V(4, 6)],
-    2: [D, D, D, D],
-    3: [V(4, 4), D, D, D],
-    4: [H, H],
-    5: [H, H],
-    6: [H, H],
-    7: [D, D, D, D],
-    8: [V(5, 2), V(5, 3), V(5, 7), V(5, 2)],
-    9: [H, H],
-    10: [D, D, D, D],
-    11: [D, D, D, D],
-    12: [V(5, 6), V(5, 6), V(5, 6), V(5, 6)],
-    13: [H, H],
-    15: [V(7, 2), D, V(7, 2), D],
-    16: [D, D, D, D],
-    17: [V(4, 2), V(6, 3), V(4, 3), V(4, 2)],
-    18: [D, D, D, D],
-    19: [H, H],
-    20: [V(4, 3), V(6, 3), V(4, 6), V(6, 3)],
-    21: [V(6, 6), V(6, 7), V(6, 6), V(6, 7)],
-    22: [V(4, 7), D, D, D],
-    23: [D, D, D, D],
-    24: [V(7, 6), V(7, 3), V(7, 6), V(7, 6)],
-    25: [H, H],
-    26: [D, D, D, D],
-    27: [D, D, D, D],
-    28: [H, H],
-    29: [D, D, D, D],
-    30: [H, H],
-    31: [D, D, D, D],
+    0: "246 242 246 247", 1: "243 246 243 246", 2: "2-- 2-- 2-- 2--", 3: "244 2-- 2-- 2--",
+    4: "4-- 4--", 5: "4-- 4--", 6: "4-- 4--", 7: "2-- 2-- 2-- 2--",
+    8: "252 253 257 252", 9: "4-- 4--", 10: "2-- 2-- 2-- 2--", 11: "2-- 2-- 2-- 2--",
+    12: "256 256 256 256", 13: "4-- 4--", 15: "272 2-- 272 2--",
+    16: "2-- 2-- 2-- 2--", 17: "242 263 243 242", 18: "2-- 2-- 2-- 2--", 19: "4-- 4--",
+    20: "243 263 246 263", 21: "266 267 266 267", 22: "247 2-- 2-- 2--", 23: "2-- 2-- 2-- 2--",
+    24: "276 273 276 276", 25: "4-- 4--", 26: "2-- 2-- 2-- 2--", 27: "2-- 2-- 2-- 2--",
+    28: "4-- 4--", 29: "2-- 2-- 2-- 2--", 30: "4-- 4--", 31: "2-- 2-- 2-- 2--",
 }
+
+
+def pieces(s):
+    return [(int(w[0]), () if w[1] == "-" else (int(w[1]) * 8 + int(w[2]),)) for w in ROUTES[s].split()]
+
 
 T_LOAD = 0.5
 T_CHIP = (1.0, 0.25)
@@ -61,7 +28,10 @@ T_LINK = (1.5, 0.75)
 
 
 def engines(src, dst):
-    return comms_topo.mask(src, dst)
+    a, b = comms_topo.chip(src), comms_topo.chip(dst)
+    if a == b:
+        return 0xFFFF
+    return 0x000F if (a & 1) == (b & 1) else 0x00F0
 
 
 def popcount(m):
@@ -69,10 +39,8 @@ def popcount(m):
 
 
 def build():
-    nbuf = {}
-    nsem = {}
+    nbuf, nsem, widths = {}, {}, {}
     loads, sends, stores = {}, {}, {}
-    widths = {}
 
     def buf(core, n):
         i = nbuf.get((core, n), 0)
@@ -91,20 +59,18 @@ def build():
         if src == dst:
             continue
         off = 0
-        for n, relays in ROUTES[s]:
+        for n, relays in pieces(s):
             path = [src] + list(relays) + [dst]
             p = {"off": off, "n": n, "path": path,
-                 "buf": [buf(c, n) for c in path], "sem": [sem(c) for c in path], "cnt": [16], "t": []}
+                 "buf": [buf(c, n) for c in path], "sem": [sem(c) for c in path], "cnt": [16]}
             off += n
             t = T_LOAD * off
-            p["t"].append(t)
             for h in range(len(path) - 1):
                 a, b = path[h], path[h + 1]
                 p["cnt"].append(popcount(engines(a, b)))
                 fix, per = T_CHIP if comms_topo.chip(a) == comms_topo.chip(b) else T_LINK
                 sends.setdefault(a, []).append((t, order, p, h))
                 t += fix + per * n
-                p["t"].append(t)
             loads.setdefault(src, []).append(p)
             stores.setdefault(dst, []).append((t, order, p))
             order += 1

@@ -16,6 +16,9 @@ ROUTES = {
     24: "276 273 276 276", 25: "4-- 4--", 26: "2-- 2-- 2-- 2--", 27: "2-- 2-- 2-- 2--",
     28: "4-- 4--", 29: "2-- 2-- 2-- 2--", 30: "4-- 4--", 31: "2-- 2-- 2-- 2--",
 }
+GATES = {48: (49,)}
+WIDE = True
+HIGH = True
 
 
 def pieces(s):
@@ -27,11 +30,9 @@ T_CHIP = (1.0, 0.25)
 T_LINK = (1.5, 0.75)
 
 
-def engines(src, dst):
+def kind(src, dst):
     a, b = comms_topo.chip(src), comms_topo.chip(dst)
-    if a == b:
-        return 0xFFFF
-    return 0x000F if (a & 1) == (b & 1) else 0x00F0
+    return "chip" if a == b else "switch" if (a & 1) == (b & 1) else "mate"
 
 
 def popcount(m):
@@ -61,14 +62,13 @@ def build():
         off = 0
         for n, relays in pieces(s):
             path = [src] + list(relays) + [dst]
-            p = {"off": off, "n": n, "path": path,
-                 "buf": [buf(c, n) for c in path], "sem": [sem(c) for c in path], "cnt": [16]}
+            p = {"off": off, "n": n, "path": path, "mask": [0] * len(path),
+                 "buf": [buf(c, n) for c in path], "sem": [sem(c) for c in path]}
             off += n
             t = T_LOAD * off
             for h in range(len(path) - 1):
                 a, b = path[h], path[h + 1]
-                p["cnt"].append(popcount(engines(a, b)))
-                fix, per = T_CHIP if comms_topo.chip(a) == comms_topo.chip(b) else T_LINK
+                fix, per = T_CHIP if kind(a, b) == "chip" else T_LINK
                 sends.setdefault(a, []).append((t, order, p, h))
                 t += fix + per * n
             loads.setdefault(src, []).append(p)
@@ -79,11 +79,22 @@ def build():
     for table in (sends, stores):
         for c in table:
             table[c].sort(key=lambda e: (e[0], e[1]))
+    for c in sends:
+        kinds = set(kind(c, p["path"][h + 1]) for t, o, p, h in sends[c])
+        for t, o, p, h in sends[c]:
+            k = kind(c, p["path"][h + 1])
+            if k == "chip":
+                m = 0xFF00 if HIGH and len(kinds) > 1 else 0xFFFF
+            elif WIDE and len(kinds - set(["chip"])) == 1:
+                m = 0x00FF
+            else:
+                m = 0x000F if k == "switch" else 0x00F0
+            p["mask"][h + 1] = m
     scratch = {}
     for n in widths:
         for i in range(widths[n]):
             scratch["b%d_%d" % (n, i)] = ("dram", [128, n * UCOLS], "float32")
-    sems = ["s%d" % i for i in range(max(nsem.values()))] + ["sent", "stored"]
+    sems = ["s%d" % i for i in range(max(nsem.values()))] + ["sent", "stored", "gate"]
     return loads, sends, stores, scratch, sems
 
 
@@ -105,18 +116,28 @@ def rank_program(g, core, T, topo):
     for i, p in enumerate(LOADS.get(core, [])):
         r0 = p["off"] * UROWS
         queues[i % 2].dma_start(T[p["buf"][0]][:], T.x[r0:r0 + p["n"] * UROWS, :]).then_inc(T.sem[p["sem"][0]], 16)
+    mine = SENDS.get(core, [])
+    first = [len(p["path"]) == 3 and h == 0 and kind(core, p["path"][1]) == "switch" for t, o, p, h in mine]
+    opens = [c for c in sorted(GATES) if core in GATES[c]]
     sent = 0
-    for t, o, p, h in SENDS.get(core, []):
+    if core in GATES:
+        g.wait_ge(T.sem.gate, len(GATES[core]))
+    for i, (t, o, p, h) in enumerate(mine):
         nxt = p["path"][h + 1]
         rid, pid, se = topo.addr(nxt)
-        m = engines(core, nxt)
-        g.wait_ge(T.sem[p["sem"][h]], p["cnt"][h])
+        m = p["mask"][h + 1]
+        g.wait_ge(T.sem[p["sem"][h]], popcount(p["mask"][h]) if h else 16)
         g.remote_dma(T[p["buf"][h + 1]][:], T[p["buf"][h]][:], T.sem[p["sem"][h + 1]], T.sem.sent, pid, rid, m)
         sent += popcount(m)
+        if first[i] and not any(first[i + 1:]):
+            for c in opens:
+                rid, pid, se = topo.addr(c)
+                g.remote_sem_update(T.sem.gate, T.sem.sent, pid, rid, 0x8000)
+                sent += 1
     for i, (t, o, p) in enumerate(STORES.get(core, [])):
         r0 = p["off"] * UROWS
         q = queues[i % 2]
-        q.wait_ge(T.sem[p["sem"][-1]], p["cnt"][-1])
+        q.wait_ge(T.sem[p["sem"][-1]], popcount(p["mask"][-1]))
         q.dma_start(T.y[r0:r0 + p["n"] * UROWS, :], T[p["buf"][-1]][:]).then_inc(T.sem.stored, 16)
         stored += 16
     g.wait_ge(T.sem.sent, sent)

@@ -17,8 +17,6 @@ ROUTES = {
     28: "4-- 4--", 29: "2-- 2-- 2-- 2--", 30: "4-- 4--", 31: "2-- 2-- 2-- 2--",
 }
 GATES = {48: (49,)}
-WIDE = True
-HIGH = True
 
 
 def pieces(s):
@@ -84,8 +82,8 @@ def build():
         for t, o, p, h in sends[c]:
             k = kind(c, p["path"][h + 1])
             if k == "chip":
-                m = 0xFF00 if HIGH and len(kinds) > 1 else 0xFFFF
-            elif WIDE and len(kinds - set(["chip"])) == 1:
+                m = 0xFF00 if len(kinds) > 1 else 0xFFFF
+            elif len(kinds - set(["chip"])) == 1:
                 m = 0x00FF
             else:
                 m = 0x000F if k == "switch" else 0x00F0

import comms_topo

UNITS = 8
UROWS = 128 // UNITS
UCOLS = 1024 // UNITS
BASE = 32
DEST = [25, 28, 20, 19, 5, 3, 7, 22, 1, 12, 26, 0, 6, 8, 14, 21, 4, 11, 30, 17, 9, 29, 10, 2, 23, 24, 15, 18, 31, 13,
        27, 16]
ROUTES = {
    0: "246 242 246 247", 1: "243 246 243 246", 2: "2-- 2-- 2-- 2--", 3: "244 2-- 2-- 2--",
    4: "4-- 4--", 5: "4-- 4--", 6: "4-- 4--", 7: "2-- 2-- 2-- 2--",
    8: "252 253 257 252", 9: "4-- 4--", 10: "2-- 2-- 2-- 2--", 11: "2-- 2-- 2-- 2--",
    12: "256 256 256 256", 13: "4-- 4--", 15: "272 2-- 272 2--",
    16: "2-- 2-- 2-- 2--", 17: "242 263 243 242", 18: "2-- 2-- 2-- 2--", 19: "4-- 4--",
    20: "243 263 246 263", 21: "266 267 266 267", 22: "247 2-- 2-- 2--", 23: "2-- 2-- 2-- 2--",
    24: "276 273 276 276", 25: "4-- 4--", 26: "2-- 2-- 2-- 2--", 27: "2-- 2-- 2-- 2--",
    28: "4-- 4--", 29: "2-- 2-- 2-- 2--", 30: "4-- 4--", 31: "2-- 2-- 2-- 2--",
}
GATES = {48: (49,)}


def pieces(s):
    return [(int(w[0]), () if w[1] == "-" else (int(w[1]) * 8 + int(w[2]),)) for w in ROUTES[s].split()]


T_LOAD = 0.5
T_CHIP = (1.0, 0.25)
T_LINK = (1.5, 0.75)


def kind(src, dst):
    a, b = comms_topo.chip(src), comms_topo.chip(dst)
    return "chip" if a == b else "switch" if (a & 1) == (b & 1) else "mate"


def popcount(m):
    return bin(m).count("1")


def build():
    nbuf, nsem, widths = {}, {}, {}
    loads, sends, stores = {}, {}, {}

    def buf(core, n):
        i = nbuf.get((core, n), 0)
        nbuf[(core, n)] = i + 1
        widths[n] = max(widths.get(n, 0), i + 1)
        return "b%d_%d" % (n, i)

    def sem(core):
        i = nsem.get(core, 0)
        nsem[core] = i + 1
        return "s%d" % i

    order = 0
    for s in range(len(DEST)):
        src, dst = BASE + s, BASE + DEST[s]
        if src == dst:
            continue
        off = 0
        for n, relays in pieces(s):
            path = [src] + list(relays) + [dst]
            p = {"off": off, "n": n, "path": path, "mask": [0] * len(path),
                 "buf": [buf(c, n) for c in path], "sem": [sem(c) for c in path]}
            off += n
            t = T_LOAD * off
            for h in range(len(path) - 1):
                a, b = path[h], path[h + 1]
                fix, per = T_CHIP if kind(a, b) == "chip" else T_LINK
                sends.setdefault(a, []).append((t, order, p, h))
                t += fix + per * n
            loads.setdefault(src, []).append(p)
            stores.setdefault(dst, []).append((t, order, p))
            order += 1
        if off != UNITS:
            raise ValueError("rank %d: pieces do not add up to a message" % s)
    for table in (sends, stores):
        for c in table:
            table[c].sort(key=lambda e: (e[0], e[1]))
    for c in sends:
        kinds = set(kind(c, p["path"][h + 1]) for t, o, p, h in sends[c])
        for t, o, p, h in sends[c]:
            k = kind(c, p["path"][h + 1])
            if k == "chip":
                m = 0xFF00 if len(kinds) > 1 else 0xFFFF
            elif len(kinds - set(["chip"])) == 1:
                m = 0x00FF
            else:
                m = 0x000F if k == "switch" else 0x00F0
            p["mask"][h + 1] = m
    scratch = {}
    for n in widths:
        for i in range(widths[n]):
            scratch["b%d_%d" % (n, i)] = ("dram", [128, n * UCOLS], "float32")
    sems = ["s%d" % i for i in range(max(nsem.values()))] + ["sent", "stored", "gate"]
    return loads, sends, stores, scratch, sems


LOADS, SENDS, STORES, SCRATCH, SEMAPHORES = build()


def rank_program(g, core, T, topo):
    rank = T.rank_of(core)
    if rank is None:
        return
    for s, d in T.tables["PERM"]:
        if DEST[s] != d:
            raise ValueError("ROUTES were laid out for another permutation")
    queues = (g.sync, g.scalar)
    stored = 0
    if DEST[rank] == rank:
        g.sync.dma_start(T.y[:], T.x[:]).then_inc(T.sem.stored, 16)
        stored += 16
    for i, p in enumerate(LOADS.get(core, [])):
        r0 = p["off"] * UROWS
        queues[i % 2].dma_start(T[p["buf"][0]][:], T.x[r0:r0 + p["n"] * UROWS, :]).then_inc(T.sem[p["sem"][0]], 16)
    mine = SENDS.get(core, [])
    first = [len(p["path"]) == 3 and h == 0 and kind(core, p["path"][1]) == "switch" for t, o, p, h in mine]
    opens = [c for c in sorted(GATES) if core in GATES[c]]
    sent = 0
    if core in GATES:
        g.wait_ge(T.sem.gate, len(GATES[core]))
    for i, (t, o, p, h) in enumerate(mine):
        nxt = p["path"][h + 1]
        rid, pid, se = topo.addr(nxt)
        m = p["mask"][h + 1]
        g.wait_ge(T.sem[p["sem"][h]], popcount(p["mask"][h]) if h else 16)
        g.remote_dma(T[p["buf"][h + 1]][:], T[p["buf"][h]][:], T.sem[p["sem"][h + 1]], T.sem.sent, pid, rid, m)
        sent += popcount(m)
        if first[i] and not any(first[i + 1:]):
            for c in opens:
                rid, pid, se = topo.addr(c)
                g.remote_sem_update(T.sem.gate, T.sem.sent, pid, rid, 0x8000)
                sent += 1
    for i, (t, o, p) in enumerate(STORES.get(core, [])):
        r0 = p["off"] * UROWS
        q = queues[i % 2]
        q.wait_ge(T.sem[p["sem"][-1]], popcount(p["mask"][-1]))
        q.dma_start(T.y[r0:r0 + p["n"] * UROWS, :], T[p["buf"][-1]][:]).then_inc(T.sem.stored, 16)
        stored += 16
    g.wait_ge(T.sem.sent, sent)
    g.wait_ge(T.sem.stored, stored)
